import numpy as np
import ml_dtypes


def mxq(x, axis, fmt="e4m3"):
    dtype, down = {"e4m3": (ml_dtypes.float8_e4m3fn, 7), "e5m2": (ml_dtypes.float8_e5m2, 14)}[fmt]
    v = np.moveaxis(np.asarray(x, np.float32).astype(ml_dtypes.bfloat16).astype(np.float64), axis, -1)
    blocks = v.reshape(v.shape[:-1] + (-1, 32))
    amax = np.abs(blocks).max(-1, keepdims=True)
    byte = np.maximum(np.where(amax > 0, np.frexp(amax)[1] - 1 + 127, 0) - down, 1)
    scale = np.exp2(byte - 127.0)
    codes = (blocks / scale).astype(np.float32).astype(dtype).astype(np.float64)
    return np.moveaxis((codes * scale).reshape(v.shape), -1, axis)


WIDE = False


def mx_kscale(k):
    if not WIDE:
        return np.ones(k)
    levels = np.array([10, -10, 5, -5, 0])
    if k % 512:
        return np.exp2(np.random.permutation(np.resize(levels, k // 32))).repeat(32)
    a = np.empty((k // 512, 16))
    for p in range(k // 512):
        a[p, :8] = np.random.permutation(np.resize(levels, 8))
        for g in range(8):
            far = levels[np.abs(levels - a[p, g]) >= 10]
            a[p, g + 8] = far[np.random.randint(len(far))]
    return np.exp2(a.ravel()).repeat(32)


def f64(x):
    return np.asarray(x).astype(np.float64)


def striped(idx):
    return np.tile(np.asarray(idx).reshape(-1, 16).T, (8, 1)).astype(np.uint16)


def unstriped(offs):
    return offs[:16].T.reshape(-1).astype(np.int64)


E2M1 = np.array([0.0, 0.5, 1.0, 1.5, 2.0, 3.0, 4.0, 6.0, -0.0, -0.5, -1.0, -1.5, -2.0, -3.0, -4.0, -6.0])


def pack_weight(w, fmt):
    k, n = w.shape
    w = f64(np.asarray(w, np.float32).astype(ml_dtypes.bfloat16)).reshape(k // 32, 32, n)
    amax = np.abs(w).max(1)
    if fmt == "e4m3":
        byte = np.frexp(amax)[1] - 1 + 127 - 7
    else:
        mant, ex = np.frexp(amax / 6.0)
        byte = np.where(mant > 0.5, ex, ex - 1) + 127
    byte = np.clip(np.where(amax > 0, byte, 1), 1, 254)
    scaled = (w * np.exp2(127.0 - byte)[:, None, :]).reshape(k, n).astype(np.float32)
    by_word = np.ascontiguousarray(scaled.reshape(k // 512, 128, 4, n).transpose(0, 1, 3, 2))
    if fmt == "e4m3":
        words = by_word.astype(ml_dtypes.float8_e4m3fn).view(np.uint8)
    else:
        c = by_word.astype(ml_dtypes.float4_e2m1fn).view(np.uint8) & 0xF
        words = (c[..., 0::2] | (c[..., 1::2] << 4)).reshape(k // 512, 128, 2 * n)
    return np.ascontiguousarray(words), np.ascontiguousarray(byte.astype(np.uint8).reshape(k // 512, 16, n))


def unpack_weight(words, scales, fmt):
    g, _, n = scales.shape
    words = np.ascontiguousarray(words).reshape(g, 128, n, -1)
    if fmt == "e4m3":
        vals = words.view(ml_dtypes.float8_e4m3fn).astype(np.float64)
    else:
        nib = np.empty((g, 128, n, 4), np.uint8)
        nib[..., 0::2] = words & 0xF
        nib[..., 1::2] = words >> 4
        vals = E2M1[nib]
    vals = vals * np.repeat(np.exp2(scales.astype(np.float64) - 127.0), 8, axis=1)[..., None]
    return vals.transpose(0, 1, 3, 2).reshape(g * 512, n)


def bf(x):
    return np.asarray(x, np.float32).astype(ml_dtypes.bfloat16)


def planes(Y):
    r, m = Y.shape
    b = f64(bf(Y)).reshape(r // 32, 32, m)
    amax = np.abs(b).max(1)
    byte = np.clip(np.where(amax > 0, np.frexp(amax)[1] - 1 + 127 - 7, 1), 1, 254)
    codes = (b * np.exp2(127.0 - byte)[:, None, :]).reshape(r, m).astype(np.float32).astype(ml_dtypes.float8_e4m3fn).view(np.uint8)
    words = codes.reshape(r // 512, 128, 4, m).transpose(0, 1, 3, 2)
    return np.ascontiguousarray(words), np.ascontiguousarray(byte.astype(np.uint8).reshape(r // 512, 16, m))


K, T, J, N = 1024, 2048, 512, 512


def setup_inputs():
    n = np.random.standard_normal
    idx = np.random.permutation(T)[:J]
    idx2 = np.random.permutation(T)[:J]
    fk = mx_kscale(K)
    wap = pack_weight(n((K, N)) * 1 / np.sqrt(K) * fk[:, None], "e2m1")
    wbp = pack_weight(n((K, N)) * 1 / np.sqrt(K) * fk[:, None], "e4m3")
    return {
        "xt": (n((K, T)) / fk[:, None]).astype(np.float32),
        "wa_words": wap[0],
        "wa_scales": wap[1],
        "wb_words": wbp[0],
        "wb_scales": wbp[1],
        "offs": striped(idx),
        "offs2": striped(idx2),
    }


def reference(xt, wa_words, wa_scales, wb_words, wb_scales, offs, offs2):
    idx = unstriped(offs)
    idx2 = unstriped(offs2)
    wau = unpack_weight(wa_words, wa_scales, "e2m1")
    wbu = unpack_weight(wb_words, wb_scales, "e4m3")
    xtidxq = mxq(f64(xt)[:, idx], 0, "e4m3")
    p = wau.T @ xtidxq
    xtidx2q = mxq(f64(xt)[:, idx2], 0, "e4m3")
    q = wbu.T @ xtidx2q
    y = p * q / (1.0 + np.abs(q))
    words, scales = planes(y)
    return y, words, scales

@@ -1,0 +1,213 @@
+from contextlib import ExitStack
+
+import concourse.mybir as mybir
+
+K, T, J, N = 1024, 2048, 512, 512
+FLOPS = 2 * 2 * K * J * N
+
+F32 = mybir.dt.float32
+BF16 = mybir.dt.bfloat16
+I32 = mybir.dt.int32
+U32 = mybir.dt.uint32
+U16 = mybir.dt.uint16
+U8 = mybir.dt.uint8
+E4M3X4 = mybir.dt.float8_e4m3fn_x4
+E2M1X4 = mybir.dt.float4_e2m1fn_x4
+ACT = mybir.ActivationFunctionType
+MULT = mybir.AluOpType.mult
+
+P = 128
+PASSES = K // 512
+QW = 128
+QUARTERS = J // QW
+
+CHUNKS = {
+    (0, 0): [(0, 1024, 0), (1024, 1024, 640)],
+    (0, 1): [(0, 1024, 0), (1024, 1024, 704)],
+    (1, 0): [(0, 512, 0), (512, 512, 0), (1024, 512, 0), (1536, 512, 64)],
+    (1, 1): [(0, 512, 0), (512, 512, 0), (1024, 512, 0), (1536, 512, 384)],
+}
+OVERLAP = 64
+PIECES = (1, 2)
+
+
+def tile_list_product_of_two_picks_pl_kernel(
+    tc, xt, wa_words, wa_scales, wb_words, wb_scales, offs, offs2, out_0, out_1, out_2
+):
+    nc = tc.nc
+    with ExitStack() as ctx:
+        pool = ctx.enter_context(tc.tile_pool(name="keep", bufs=1))
+        psum = ctx.enter_context(tc.psum_pool(name="psum", bufs=1))
+
+        def tile(shape, dtype, name, tag=None):
+            return pool.tile(shape, dtype, name=name, tag=tag or name, align_bytes=64)
+
+        list_a = tile([P, J // 16], U16, "list_a")
+        list_b = tile([P, J // 16], U16, "list_b")
+        lists = {"a": list_a, "b": list_b}
+
+        unit = tile([P, 1], F32, "unit")
+        nc.vector.memset(unit[:], 1.0)
+        one = tile([P, 1], F32, "one")
+        nc.scalar.activation(one[:], unit[:], ACT.Abs_reciprocal_sqrt)
+
+        sc_raw = tile([P, PASSES, N // 4], I32, "sc_raw")
+        nc.vector.memset(sc_raw[:], 0)
+        wb_raw = tile([P, PASSES, N], I32, "wb_raw")
+        wa_raw = tile([P, PASSES, N // 2], I32, "wa_raw")
+
+        raw = {}
+
+        def load_chunk(z, u, i):
+            c0, w, v = CHUNKS[z, u][i]
+            rows = xt[512 * z : 512 * (z + 1), :].rearrange("(p u e) t -> p u e t", u=2, e=2)
+            raw[z, u, c0] = tile([P, 2, w], F32, f"raw{z}{u}_{c0}")
+            nc.sync.dma_start(raw[z, u, c0][:], rows[:, u, :, c0 : c0 + w])
+
+        def load_scales(q):
+            for base, src in ((0, wa_scales), (4, wb_scales)):
+                nc.sync.dma_start(
+                    sc_raw[32 * q + base : 32 * q + base + 4, :, :],
+                    src[:, 4 * q : 4 * q + 4, :].rearrange("z r n -> r z n").bitcast(I32),
+                )
+
+        nc.sync.dma_start(wb_raw[:], wb_words.rearrange("z p n r -> p z (n r)").bitcast(I32))
+        load_scales(0)
+        load_scales(1)
+        nc.sync.dma_start(wa_raw[:], wa_words.rearrange("z p b -> p z b").bitcast(I32))
+        load_chunk(0, 0, 0)
+        load_chunk(0, 0, 1)
+        nc.sync.dma_start(list_b[:], offs2)
+        nc.sync.dma_start(list_a[:], offs)
+        load_scales(2)
+        load_scales(3)
+        for z, u in ((0, 1), (1, 0), (1, 1)):
+            for i in range(len(CHUNKS[z, u])):
+                load_chunk(z, u, i)
+
+        wb = tile([P, PASSES, 4, P], I32, "wb")
+        wa = tile([P, PASSES, 4, P], U16, "wa")
+        nc.vector.tensor_copy(
+            wb[:].rearrange("p z t m -> p z m t"), wb_raw[:].rearrange("p z (m t) -> p z m t", t=4)
+        )
+        nc.vector.tensor_copy(
+            wa[:].rearrange("p z t m -> p z m t"),
+            wa_raw[:].bitcast(U16).rearrange("p z (m t) -> p z m t", t=4),
+        )
+
+        banks = {
+            (s, c): psum.tile([P, 4, QW], F32, name=f"bank_{s}{c}") for s in "ba" for c in range(QUARTERS)
+        }
+
+        picked, quantised = {}, {}
+        windows = tile([P, 2 * (4 * T - 3 * OVERLAP)], BF16, "windows")
+
+        def gather_pair(z, u):
+            width = J // PIECES[z]
+            first = (3 - 2 * z - u) * (T - OVERLAP)
+            pairs = windows[:, 2 * first : 2 * (first + T)]
+            for c0, w, v in CHUNKS[z, u]:
+                src = raw[z, u, c0]
+                dst = pairs[:, 2 * c0 : 2 * (c0 + w)].rearrange("p (c e) -> p c e", e=2)
+                nc.scalar.activation(
+                    dst[:, : w - v, :], src[:, :, : w - v].rearrange("p e c -> p c e"), ACT.Copy
+                )
+                if v:
+                    nc.vector.tensor_copy(dst[:, w - v :, :], src[:, :, w - v :].rearrange("p e c -> p c e"))
+            for h in range(PIECES[z]):
+                for s in "ba":
+                    if u == 0 and h == 0:
+                        picked[z, s] = tile([P, PIECES[z] + 1, width], F32, f"picked{z}{s}")
+                    cols = slice(h * width // 16, (h + 1) * width // 16)
+                    row = h if u == 0 else PIECES[z]
+                    nc.vector.tensor_copy(
+                        picked[z, s][:, row, :], pairs.bitcast(F32).indirect(lists[s][:, cols])
+                    )
+                if u == 1:
+                    for s in "ba":
+                        quantise(z, s, h)
+                    for s in "ba":
+                        multiply(z, s, h, sc)
+
+        def quantise(z, s, h):
+            width = J // PIECES[z]
+            woven = tile([P, width, 2], F32, f"woven{z}{s}{h}")
+            src = picked[z, s][:, h :: PIECES[z] - h, :].rearrange("p u j -> p j u")
+            if (z, s, h) != (1, "a", 0):
+                nc.vector.tensor_copy(woven[:], src)
+            else:
+                nc.scalar.copy(woven[:], src)
+            codes = tile([P, width], U32, f"codes{z}{s}{h}")
+            scales = tile([P, width], U8, f"scales{z}{s}{h}")
+            nc.vector.quantize_mx(
+                out=codes[:].bitcast(E4M3X4),
+                scales=scales[:],
+                in_=woven[:].rearrange("p j u -> p (j u)").bitcast(BF16),
+            )
+            quantised[z, s, h] = (codes, scales)
+
+        def multiply(z, s, h, sc):
+            width = J // PIECES[z]
+            codes, scales = quantised[z, s, h]
+            for cc in range(width // QW):
+                c = h * width // QW + cc
+                cols = slice(cc * QW, (cc + 1) * QW)
+                for t in range(4):
+                    if s == "a":
+                        lhsT = wa[:, z, t, :].bitcast(U8).bitcast(E2M1X4)
+                        lhsT_scale = sc[:, z, t, :]
+                    else:
+                        lhsT = wb[:, z, t, :].bitcast(E4M3X4)
+                        lhsT_scale = sc[4:, z, t, :]
+                    nc.tensor.matmul_mx(
+                        out=banks[s, c][:, t, :],
+                        lhsT=lhsT,
+                        lhsT_scale=lhsT_scale,
+                        rhs=codes[:, cols].bitcast(E4M3X4),
+                        rhs_scale=scales[:, cols],
+                        start=(z == 0 and t == 0),
+                        stop=(z == PASSES - 1 and t == 3),
+                    )
+
+        sc = tile([P, PASSES, 4, P], U8, "sc")
+        nc.vector.tensor_copy(
+            sc[:].rearrange("p z t m -> p z m t"),
+            sc_raw[:].bitcast(U8).rearrange("p z (m t) -> p z m t", t=4),
+        )
+        for z in range(PASSES):
+            for u in range(2):
+                gather_pair(z, u)
+
+        y_codes = tile([P, J], U32, "y_codes")
+        y_scales = tile([P, J], U8, "y_scales")
+        out_rows = out_0.rearrange("(p t) j -> p t j", t=4)
+        out_words = out_1[0].rearrange("p j r -> p (j r)").bitcast(I32)
+        for c in range(QUARTERS):
+            cols = slice(c * QW, (c + 1) * QW)
+            mag = tile([P, 4, QW], F32, f"mag{c}")
+            nc.scalar.activation(mag[:], banks["b", c][:], ACT.Abs)
+            root = tile([P, 4, QW], F32, f"root{c}")
+            nc.scalar.activation(root[:], mag[:], ACT.Abs_reciprocal_sqrt, bias=one[:])
+            recip = tile([P, 4, QW], F32, f"recip{c}")
+            nc.scalar.activation(recip[:], root[:], ACT.Square)
+            soft = tile([P, 4, QW], F32, f"soft{c}")
+            nc.vector.tensor_tensor(soft[:], banks["b", c][:], recip[:], MULT)
+            y = tile([P, 4, QW], F32, f"y{c}")
+            nc.vector.tensor_tensor(y[:], banks["a", c][:], soft[:], MULT)
+            nc.sync.dma_start(out_rows[:, :, cols], y[:])
+            yb = tile([P, QW, 4], BF16, f"yb{c}")
+            if c == 2:
+                nc.scalar.copy(yb[:], y[:].rearrange("p t j -> p j t"))
+            else:
+                nc.vector.tensor_copy(yb[:], y[:].rearrange("p t j -> p j t"))
+            nc.vector.quantize_mx(
+                out=y_codes[:, cols].bitcast(E4M3X4),
+                scales=y_scales[:, cols],
+                in_=yb[:].rearrange("p j t -> p (j t)"),
+            )
+            nc.sync.dma_start(out_words[:, cols], y_codes[:, cols].bitcast(I32))
+        for q in range(4):
+            eng = nc.sync if q % 2 == 0 else nc.scalar
+            eng.dma_start(
+                out_2[0, 4 * q : 4 * q + 4, :].bitcast(I32), y_scales[32 * q : 32 * q + 4, :].bitcast(I32)
+            )

@@ -22,13 +22,21 @@ QW = 128
 QUARTERS = J // QW
 
 CHUNKS = {
-    (0, 0): [(0, 1024, 0), (1024, 1024, 640)],
+    (0, 0): [(0, 2048, 1280)],
     (0, 1): [(0, 1024, 0), (1024, 1024, 704)],
-    (1, 0): [(0, 512, 0), (512, 512, 0), (1024, 512, 0), (1536, 512, 64)],
-    (1, 1): [(0, 512, 0), (512, 512, 0), (1024, 512, 0), (1536, 512, 384)],
+    (1, 0): [(0, 1024, 0), (1024, 1024, 256)],
+    (1, 1): [(0, 1024, 0), (1024, 512, 384), (1536, 512, 320)],
 }
-OVERLAP = 64
+OVERLAP = 576
 PIECES = (1, 2)
+ROWS = {
+    (0, "b", 0): (0, 2),
+    (0, "a", 0): (1, 3),
+    (1, "b", 0): (0, 4),
+    (1, "a", 0): (2, 5),
+    (1, "b", 1): (1, 2),
+    (1, "a", 1): (3, 5),
+}
 
 
 def tile_list_product_of_two_picks_pl_kernel(
@@ -71,29 +79,43 @@ def tile_list_product_of_two_picks_pl_kernel(
                     src[:, 4 * q : 4 * q + 4, :].rearrange("z r n -> r z n").bitcast(I32),
                 )
 
-        nc.sync.dma_start(wb_raw[:], wb_words.rearrange("z p n r -> p z (n r)").bitcast(I32))
-        load_scales(0)
-        load_scales(1)
-        nc.sync.dma_start(wa_raw[:], wa_words.rearrange("z p b -> p z b").bitcast(I32))
         load_chunk(0, 0, 0)
-        load_chunk(0, 0, 1)
         nc.sync.dma_start(list_b[:], offs2)
         nc.sync.dma_start(list_a[:], offs)
+        load_scales(0)
+        load_scales(1)
+        load_chunk(0, 1, 0)
         load_scales(2)
         load_scales(3)
-        for z, u in ((0, 1), (1, 0), (1, 1)):
-            for i in range(len(CHUNKS[z, u])):
-                load_chunk(z, u, i)
+        load_chunk(0, 1, 1)
+        load_chunk(1, 0, 0)
+        load_chunk(1, 0, 1)
+        nc.sync.dma_start(wb_raw[:], wb_words.rearrange("z p n r -> p z (n r)").bitcast(I32))
+        nc.sync.dma_start(wa_raw[:], wa_words.rearrange("z p b -> p z b").bitcast(I32))
+        for i in range(len(CHUNKS[1, 1])):
+            load_chunk(1, 1, i)
 
-        wb = tile([P, PASSES, 4, P], I32, "wb")
-        wa = tile([P, PASSES, 4, P], U16, "wa")
-        nc.vector.tensor_copy(
-            wb[:].rearrange("p z t m -> p z m t"), wb_raw[:].rearrange("p z (m t) -> p z m t", t=4)
-        )
-        nc.vector.tensor_copy(
-            wa[:].rearrange("p z t m -> p z m t"),
-            wa_raw[:].bitcast(U16).rearrange("p z (m t) -> p z m t", t=4),
-        )
+        dealt = {}
+
+        def deal_scales():
+            sc = tile([P, PASSES, 4, P], U8, "sc", tag="raw00_0")
+            dealt["scales"] = sc
+            nc.vector.tensor_copy(
+                sc[:].rearrange("p z t m -> p z m t"),
+                sc_raw[:].bitcast(U8).rearrange("p z (m t) -> p z m t", t=4),
+            )
+
+        def deal_weights():
+            both = tile([P, PASSES * (N + N // 2)], I32, "both", tag="raw10_1024")
+            dealt["b"] = both[:, : PASSES * N].rearrange("p (z t m) -> p z t m", z=PASSES, t=4)
+            dealt["a"] = both[:, PASSES * N :].bitcast(U16).rearrange("p (z t m) -> p z t m", z=PASSES, t=4)
+            nc.vector.tensor_copy(
+                dealt["b"].rearrange("p z t m -> p z m t"), wb_raw[:].rearrange("p z (m t) -> p z m t", t=4)
+            )
+            nc.vector.tensor_copy(
+                dealt["a"].rearrange("p z t m -> p z m t"),
+                wa_raw[:].bitcast(U16).rearrange("p z (m t) -> p z m t", t=4),
+            )
 
         banks = {
             (s, c): psum.tile([P, 4, QW], F32, name=f"bank_{s}{c}") for s in "ba" for c in range(QUARTERS)
@@ -109,55 +131,71 @@ def tile_list_product_of_two_picks_pl_kernel(
             for c0, w, v in CHUNKS[z, u]:
                 src = raw[z, u, c0]
                 dst = pairs[:, 2 * c0 : 2 * (c0 + w)].rearrange("p (c e) -> p c e", e=2)
-                nc.scalar.activation(
-                    dst[:, : w - v, :], src[:, :, : w - v].rearrange("p e c -> p c e"), ACT.Copy
-                )
+                if v < w:
+                    nc.scalar.activation(
+                        dst[:, : w - v, :], src[:, :, : w - v].rearrange("p e c -> p c e"), ACT.Copy
+                    )
                 if v:
                     nc.vector.tensor_copy(dst[:, w - v :, :], src[:, :, w - v :].rearrange("p e c -> p c e"))
+            if u == 0:
+                picked[z] = tile([P, 2 * J + 2 * width], F32, f"picked{z}")
+                for i, s in enumerate("ba"):
+                    nc.vector.tensor_copy(
+                        picked[z][:, i * J : (i + 1) * J], pairs.bitcast(F32).indirect(lists[s][:])
+                    )
+                if z == 0:
+                    deal_scales()
+                else:
+                    deal_weights()
+                    for s in "ba":
+                        multiply(0, s, 0)
+                return
             for h in range(PIECES[z]):
                 for s in "ba":
-                    if u == 0 and h == 0:
-                        picked[z, s] = tile([P, PIECES[z] + 1, width], F32, f"picked{z}{s}")
                     cols = slice(h * width // 16, (h + 1) * width // 16)
-                    row = h if u == 0 else PIECES[z]
+                    at = ROWS[z, s, h][1] * width
                     nc.vector.tensor_copy(
-                        picked[z, s][:, row, :], pairs.bitcast(F32).indirect(lists[s][:, cols])
+                        picked[z][:, at : at + width], pairs.bitcast(F32).indirect(lists[s][:, cols])
                     )
-                if u == 1:
+                for s in "ba":
+                    quantise(z, s, h)
+                if z == 1:
                     for s in "ba":
-                        quantise(z, s, h)
-                    for s in "ba":
-                        multiply(z, s, h, sc)
+                        multiply(z, s, h)
 
         def quantise(z, s, h):
             width = J // PIECES[z]
-            woven = tile([P, width, 2], F32, f"woven{z}{s}{h}")
-            src = picked[z, s][:, h :: PIECES[z] - h, :].rearrange("p u j -> p j u")
-            if (z, s, h) != (1, "a", 0):
-                nc.vector.tensor_copy(woven[:], src)
+            woven = tile([P, 2 * width], F32, f"woven{z}{s}{h}")[:]
+            r0, r1 = ROWS[z, s, h]
+            src = picked[z][:].rearrange("p (r j) -> p r j", j=width)
+            src = src[:, r0 : r1 + 1 : r1 - r0, :].rearrange("p u j -> p j u")
+            dst = woven.rearrange("p (j u) -> p j u", u=2)
+            if (z, h) != (1, 0):
+                nc.vector.tensor_copy(dst, src)
             else:
-                nc.scalar.copy(woven[:], src)
+                nc.scalar.copy(dst, src)
             codes = tile([P, width], U32, f"codes{z}{s}{h}")
             scales = tile([P, width], U8, f"scales{z}{s}{h}")
             nc.vector.quantize_mx(
                 out=codes[:].bitcast(E4M3X4),
                 scales=scales[:],
-                in_=woven[:].rearrange("p j u -> p (j u)").bitcast(BF16),
+                in_=woven.bitcast(BF16),
             )
             quantised[z, s, h] = (codes, scales)
 
-        def multiply(z, s, h, sc):
+        def multiply(z, s, h):
             width = J // PIECES[z]
             codes, scales = quantised[z, s, h]
+            sc = dealt["scales"]
             for cc in range(width // QW):
                 c = h * width // QW + cc
                 cols = slice(cc * QW, (cc + 1) * QW)
                 for t in range(4):
                     if s == "a":
-                        lhsT = wa[:, z, t, :].bitcast(U8).bitcast(E2M1X4)
+                        lhsT = dealt["a"][:, z, t, :].bitcast(U8).bitcast(E2M1X4)
                         lhsT_scale = sc[:, z, t, :]
                     else:
-                        lhsT = wb[:, z, t, :].bitcast(E4M3X4)
+                        lhsT = dealt["b"][:, z, t, :].bitcast(E4M3X4)
                         lhsT_scale = sc[4:, z, t, :]
                     nc.tensor.matmul_mx(
                         out=banks[s, c][:, t, :],
@@ -169,11 +207,6 @@ def tile_list_product_of_two_picks_pl_kernel(
                         stop=(z == PASSES - 1 and t == 3),
                     )
 
-        sc = tile([P, PASSES, 4, P], U8, "sc")
-        nc.vector.tensor_copy(
-            sc[:].rearrange("p z t m -> p z m t"),
-            sc_raw[:].bitcast(U8).rearrange("p z (m t) -> p z m t", t=4),
-        )
         for z in range(PASSES):
             for u in range(2):
                 gather_pair(z, u)
@@ -188,23 +221,28 @@ def tile_list_product_of_two_picks_pl_kernel(
             nc.scalar.activation(mag[:], banks["b", c][:], ACT.Abs)
             root = tile([P, 4, QW], F32, f"root{c}")
             nc.scalar.activation(root[:], mag[:], ACT.Abs_reciprocal_sqrt, bias=one[:])
-            recip = tile([P, 4, QW], F32, f"recip{c}")
-            nc.scalar.activation(recip[:], root[:], ACT.Square)
-            soft = tile([P, 4, QW], F32, f"soft{c}")
-            nc.vector.tensor_tensor(soft[:], banks["b", c][:], recip[:], MULT)
             y = tile([P, 4, QW], F32, f"y{c}")
-            nc.vector.tensor_tensor(y[:], banks["a", c][:], soft[:], MULT)
+            parts = 2 if c == QUARTERS - 1 else 1
+            w = QW // parts
+            for i in range(parts):
+                js = slice(i * w, (i + 1) * w)
+                recip = tile([P, 4, w], F32, f"recip{c}{i}")
+                soft = tile([P, 4, w], F32, f"soft{c}{i}")
+                nc.scalar.activation(recip[:], root[:, :, js], ACT.Square)
+                nc.vector.tensor_tensor(soft[:], banks["b", c][:, :, js], recip[:], MULT)
+                nc.vector.tensor_tensor(y[:, :, js], banks["a", c][:, :, js], soft[:], MULT)
+                yb = tile([P, w, 4], BF16, f"yb{c}{i}")
+                if (c, i) in ((2, 0), (3, 0)):
+                    nc.scalar.copy(yb[:], y[:, :, js].rearrange("p t j -> p j t"))
+                else:
+                    nc.vector.tensor_copy(yb[:], y[:, :, js].rearrange("p t j -> p j t"))
+                oc = slice(c * QW + i * w, c * QW + (i + 1) * w)
+                nc.vector.quantize_mx(
+                    out=y_codes[:, oc].bitcast(E4M3X4),
+                    scales=y_scales[:, oc],
+                    in_=yb[:].rearrange("p j t -> p (j t)"),
+                )
             nc.sync.dma_start(out_rows[:, :, cols], y[:])
-            yb = tile([P, QW, 4], BF16, f"yb{c}")
-            if c == 2:
-                nc.scalar.copy(yb[:], y[:].rearrange("p t j -> p j t"))
-            else:
-                nc.vector.tensor_copy(yb[:], y[:].rearrange("p t j -> p j t"))
-            nc.vector.quantize_mx(
-                out=y_codes[:, cols].bitcast(E4M3X4),
-                scales=y_scales[:, cols],
-                in_=yb[:].rearrange("p j t -> p (j t)"),
-            )
             nc.sync.dma_start(out_words[:, cols], y_codes[:, cols].bitcast(I32))
         for q in range(4):
             eng = nc.sync if q % 2 == 0 else nc.scalar

@@ -101,8 +101,8 @@ def tile_list_product_of_two_picks_pl_kernel(
             sc = tile([P, PASSES, 4, P], U8, "sc", tag="raw00_0")
             dealt["scales"] = sc
             nc.vector.tensor_copy(
-                sc[:].rearrange("p z t m -> p z m t"),
-                sc_raw[:].bitcast(U8).rearrange("p z (m t) -> p z m t", t=4),
+                sc[:].rearrange("p z t (g i) -> p z g t i", i=16),
+                sc_raw[:].bitcast(U8).rearrange("p z (g i t) -> p z g t i", i=16, t=4),
             )
 
         def deal_weights():
@@ -110,11 +110,12 @@ def tile_list_product_of_two_picks_pl_kernel(
             dealt["b"] = both[:, : PASSES * N].rearrange("p (z t m) -> p z t m", z=PASSES, t=4)
             dealt["a"] = both[:, PASSES * N :].bitcast(U16).rearrange("p (z t m) -> p z t m", z=PASSES, t=4)
             nc.vector.tensor_copy(
-                dealt["b"].rearrange("p z t m -> p z m t"), wb_raw[:].rearrange("p z (m t) -> p z m t", t=4)
+                dealt["b"].rearrange("p z t (g i) -> p z g t i", i=4),
+                wb_raw[:].rearrange("p z (g i t) -> p z g t i", i=4, t=4),
             )
             nc.vector.tensor_copy(
-                dealt["a"].rearrange("p z t m -> p z m t"),
-                wa_raw[:].bitcast(U16).rearrange("p z (m t) -> p z m t", t=4),
+                dealt["a"].rearrange("p z t (g i) -> p z g t i", i=8),
+                wa_raw[:].bitcast(U16).rearrange("p z (g i t) -> p z g t i", i=8, t=4),
             )
 
         banks = {
@@ -232,10 +233,12 @@ def tile_list_product_of_two_picks_pl_kernel(
                 nc.vector.tensor_tensor(soft[:], banks["b", c][:, :, js], recip[:], MULT)
                 nc.vector.tensor_tensor(y[:, :, js], banks["a", c][:, :, js], soft[:], MULT)
                 yb = tile([P, w, 4], BF16, f"yb{c}{i}")
+                src = y[:, :, js].rearrange("p t (g e) -> p g t e", e=4)
+                dst = yb[:].rearrange("p (g e) t -> p g t e", e=4)
                 if (c, i) in ((2, 0), (3, 0)):
-                    nc.scalar.copy(yb[:], y[:, :, js].rearrange("p t j -> p j t"))
+                    nc.scalar.copy(dst, src)
                 else:
-                    nc.vector.tensor_copy(yb[:], y[:, :, js].rearrange("p t j -> p j t"))
+                    nc.vector.tensor_copy(dst, src)
                 oc = slice(c * QW + i * w, c * QW + (i + 1) * w)
                 nc.vector.quantize_mx(
                     out=y_codes[:, oc].bitcast(E4M3X4),

@@ -18,17 +18,20 @@ MULT = mybir.AluOpType.mult
 
 P = 128
 PASSES = K // 512
-QW = 128
-QUARTERS = J // QW
+QUARTER = 128
+QUARTERS = J // QUARTER
+LINE = 16
+SIDES = "ba"
+WB_SCALE_ROW = 4
 
-CHUNKS = {
+LOADS = {
     (0, 0): [(0, 2048, 1280)],
     (0, 1): [(0, 1024, 0), (1024, 1024, 704)],
     (1, 0): [(0, 1024, 0), (1024, 1024, 256)],
-    (1, 1): [(0, 1024, 0), (1024, 512, 384), (1536, 512, 320)],
+    (1, 1): [(0, 1024, 0), (1024, 768, 512), (1792, 256, 256)],
 }
 OVERLAP = 576
-PIECES = (1, 2)
+HALVES = (1, 2)
 ROWS = {
     (0, "b", 0): (0, 2),
     (0, "a", 0): (1, 3),
@@ -50,205 +53,196 @@ def tile_list_product_of_two_picks_pl_kernel(
         def tile(shape, dtype, name, tag=None):
             return pool.tile(shape, dtype, name=name, tag=tag or name, align_bytes=64)
 
-        list_a = tile([P, J // 16], U16, "list_a")
-        list_b = tile([P, J // 16], U16, "list_b")
-        lists = {"a": list_a, "b": list_b}
+        lists = {"a": tile([P, J // 16], U16, "list_a"), "b": tile([P, J // 16], U16, "list_b")}
 
         unit = tile([P, 1], F32, "unit")
         nc.vector.memset(unit[:], 1.0)
         one = tile([P, 1], F32, "one")
         nc.scalar.activation(one[:], unit[:], ACT.Abs_reciprocal_sqrt)
 
-        sc_raw = tile([P, PASSES, N // 4], I32, "sc_raw")
-        nc.vector.memset(sc_raw[:], 0)
+        scales_raw = tile([P, PASSES, N // 4], I32, "scales_raw")
+        nc.vector.memset(scales_raw[:], 0)
         wb_raw = tile([P, PASSES, N], I32, "wb_raw")
         wa_raw = tile([P, PASSES, N // 2], I32, "wa_raw")
-
         raw = {}
 
-        def load_chunk(z, u, i):
-            c0, w, v = CHUNKS[z, u][i]
-            rows = xt[512 * z : 512 * (z + 1), :].rearrange("(p u e) t -> p u e t", u=2, e=2)
-            raw[z, u, c0] = tile([P, 2, w], F32, f"raw{z}{u}_{c0}")
-            nc.sync.dma_start(raw[z, u, c0][:], rows[:, u, :, c0 : c0 + w])
+        def load_tokens(z, u, i):
+            first, count, on_vector = LOADS[z, u][i]
+            rows = xt[512 * z : 512 * (z + 1), :].rearrange("(p u e) c -> p u e c", u=2, e=2)
+            raw[z, u, first] = tile([P, 2, count], F32, f"raw{z}{u}_{first}")
+            nc.sync.dma_start(raw[z, u, first][:], rows[:, u, :, first : first + count])
 
-        def load_scales(q):
-            for base, src in ((0, wa_scales), (4, wb_scales)):
+        def load_weight_scales(quadrant):
+            for row, source in ((0, wa_scales), (WB_SCALE_ROW, wb_scales)):
+                at = 32 * quadrant + row
                 nc.sync.dma_start(
-                    sc_raw[32 * q + base : 32 * q + base + 4, :, :],
-                    src[:, 4 * q : 4 * q + 4, :].rearrange("z r n -> r z n").bitcast(I32),
+                    scales_raw[at : at + 4, :, :],
+                    source[:, 4 * quadrant : 4 * quadrant + 4, :].rearrange("z r n -> r z n").bitcast(I32),
                 )
 
-        load_chunk(0, 0, 0)
-        nc.sync.dma_start(list_b[:], offs2)
-        nc.sync.dma_start(list_a[:], offs)
-        load_scales(0)
-        load_scales(1)
-        load_chunk(0, 1, 0)
-        load_scales(2)
-        load_scales(3)
-        load_chunk(0, 1, 1)
-        load_chunk(1, 0, 0)
-        load_chunk(1, 0, 1)
+        load_tokens(0, 0, 0)
+        nc.sync.dma_start(lists["b"][:], offs2)
+        nc.sync.dma_start(lists["a"][:], offs)
+        load_weight_scales(0)
+        load_weight_scales(1)
+        load_tokens(0, 1, 0)
+        load_weight_scales(2)
+        load_weight_scales(3)
+        load_tokens(0, 1, 1)
+        load_tokens(1, 0, 0)
+        load_tokens(1, 0, 1)
         nc.sync.dma_start(wb_raw[:], wb_words.rearrange("z p n r -> p z (n r)").bitcast(I32))
         nc.sync.dma_start(wa_raw[:], wa_words.rearrange("z p b -> p z b").bitcast(I32))
-        for i in range(len(CHUNKS[1, 1])):
-            load_chunk(1, 1, i)
+        for i in range(len(LOADS[1, 1])):
+            load_tokens(1, 1, i)
 
         dealt = {}
 
-        def deal_scales():
-            sc = tile([P, PASSES, 4, P], U8, "sc", tag="raw00_0")
-            dealt["scales"] = sc
+        def deal(dst, src, item_bytes):
+            run = LINE // item_bytes
             nc.vector.tensor_copy(
-                sc[:].rearrange("p z t (g i) -> p z g t i", i=16),
-                sc_raw[:].bitcast(U8).rearrange("p z (g i t) -> p z g t i", i=16, t=4),
+                dst.rearrange("p z t (g i) -> p z g t i", i=run),
+                src.rearrange("p z (g i t) -> p z g t i", i=run, t=4),
             )
 
-        def deal_weights():
-            both = tile([P, PASSES * (N + N // 2)], I32, "both", tag="raw10_1024")
+        def deal_weight_scales():
+            scales = tile([P, PASSES, 4, P], U8, "weight_scales", tag="raw00_0")
+            dealt["scales"] = scales
+            deal(scales[:], scales_raw[:].bitcast(U8), 1)
+
+        def deal_weight_codes():
+            both = tile([P, PASSES * (N + N // 2)], I32, "weight_codes", tag="raw10_1024")
             dealt["b"] = both[:, : PASSES * N].rearrange("p (z t m) -> p z t m", z=PASSES, t=4)
             dealt["a"] = both[:, PASSES * N :].bitcast(U16).rearrange("p (z t m) -> p z t m", z=PASSES, t=4)
-            nc.vector.tensor_copy(
-                dealt["b"].rearrange("p z t (g i) -> p z g t i", i=4),
-                wb_raw[:].rearrange("p z (g i t) -> p z g t i", i=4, t=4),
-            )
-            nc.vector.tensor_copy(
-                dealt["a"].rearrange("p z t (g i) -> p z g t i", i=8),
-                wa_raw[:].bitcast(U16).rearrange("p z (g i t) -> p z g t i", i=8, t=4),
-            )
+            deal(dealt["b"], wb_raw[:], 4)
+            deal(dealt["a"], wa_raw[:].bitcast(U16), 2)
 
         banks = {
-            (s, c): psum.tile([P, 4, QW], F32, name=f"bank_{s}{c}") for s in "ba" for c in range(QUARTERS)
+            (s, c): psum.tile([P, 4, QUARTER], F32, name=f"bank_{s}{c}") for s in SIDES for c in range(QUARTERS)
         }
-
-        picked, quantised = {}, {}
         windows = tile([P, 2 * (4 * T - 3 * OVERLAP)], BF16, "windows")
+        picked, quantised = {}, {}
 
-        def gather_pair(z, u):
-            width = J // PIECES[z]
-            first = (3 - 2 * z - u) * (T - OVERLAP)
-            pairs = windows[:, 2 * first : 2 * (first + T)]
-            for c0, w, v in CHUNKS[z, u]:
-                src = raw[z, u, c0]
-                dst = pairs[:, 2 * c0 : 2 * (c0 + w)].rearrange("p (c e) -> p c e", e=2)
-                if v < w:
-                    nc.scalar.activation(
-                        dst[:, : w - v, :], src[:, :, : w - v].rearrange("p e c -> p c e"), ACT.Copy
-                    )
-                if v:
-                    nc.vector.tensor_copy(dst[:, w - v :, :], src[:, :, w - v :].rearrange("p e c -> p c e"))
-            if u == 0:
-                picked[z] = tile([P, 2 * J + 2 * width], F32, f"picked{z}")
-                for i, s in enumerate("ba"):
-                    nc.vector.tensor_copy(
-                        picked[z][:, i * J : (i + 1) * J], pairs.bitcast(F32).indirect(lists[s][:])
-                    )
-                if z == 0:
-                    deal_scales()
-                else:
-                    deal_weights()
-                    for s in "ba":
-                        multiply(0, s, 0)
-                return
-            for h in range(PIECES[z]):
-                for s in "ba":
-                    cols = slice(h * width // 16, (h + 1) * width // 16)
-                    at = ROWS[z, s, h][1] * width
-                    nc.vector.tensor_copy(
-                        picked[z][:, at : at + width], pairs.bitcast(F32).indirect(lists[s][:, cols])
-                    )
-                for s in "ba":
-                    quantise(z, s, h)
-                if z == 1:
-                    for s in "ba":
-                        multiply(z, s, h)
+        def round_pair(z, u):
+            start = (3 - 2 * z - u) * (T - OVERLAP)
+            window = windows[:, 2 * start : 2 * (start + T)]
+            for first, count, on_vector in LOADS[z, u]:
+                src = raw[z, u, first][:].rearrange("p e c -> p c e")
+                dst = window[:, 2 * first : 2 * (first + count)].rearrange("p (c e) -> p c e", e=2)
+                split = count - on_vector
+                if split:
+                    nc.scalar.activation(dst[:, :split, :], src[:, :split, :], ACT.Copy)
+                if on_vector:
+                    nc.vector.tensor_copy(dst[:, split:, :], src[:, split:, :])
+            return window.bitcast(F32)
+
+        def gather_first_pair(z, window):
+            picked[z] = tile([P, 2 * J + 2 * (J // HALVES[z])], F32, f"picked{z}")
+            for i, s in enumerate(SIDES):
+                nc.vector.tensor_copy(picked[z][:, i * J : (i + 1) * J], window.indirect(lists[s][:]))
+
+        def gather_second_pair(z, window, h):
+            width = J // HALVES[z]
+            for s in SIDES:
+                at = ROWS[z, s, h][1] * width
+                entries = lists[s][:, h * width // 16 : (h + 1) * width // 16]
+                nc.vector.tensor_copy(picked[z][:, at : at + width], window.indirect(entries))
 
         def quantise(z, s, h):
-            width = J // PIECES[z]
-            woven = tile([P, 2 * width], F32, f"woven{z}{s}{h}")[:]
-            r0, r1 = ROWS[z, s, h]
-            src = picked[z][:].rearrange("p (r j) -> p r j", j=width)
-            src = src[:, r0 : r1 + 1 : r1 - r0, :].rearrange("p u j -> p j u")
-            dst = woven.rearrange("p (j u) -> p j u", u=2)
-            if (z, h) != (1, 0):
-                nc.vector.tensor_copy(dst, src)
-            else:
-                nc.scalar.copy(dst, src)
-            codes = tile([P, width], U32, f"codes{z}{s}{h}")
-            scales = tile([P, width], U8, f"scales{z}{s}{h}")
-            nc.vector.quantize_mx(
-                out=codes[:].bitcast(E4M3X4),
-                scales=scales[:],
-                in_=woven.bitcast(BF16),
-            )
-            quantised[z, s, h] = (codes, scales)
+            width = J // HALVES[z]
+            step = QUARTER if (z, s, h) == (PASSES - 1, "b", 0) else width
+            row0, row1 = ROWS[z, s, h]
+            rows = picked[z][:].rearrange("p (r j) -> p r j", j=width)[:, row0 : row1 + 1 : row1 - row0, :]
+            for j in range(0, width, step):
+                woven = tile([P, 2 * step], F32, f"woven{z}{s}{h}_{j}")
+                src = rows[:, :, j : j + step].rearrange("p u j -> p j u")
+                dst = woven[:].rearrange("p (j u) -> p j u", u=2)
+                if (z, h) == (PASSES - 1, 0):
+                    nc.scalar.copy(dst, src)
+                else:
+                    nc.vector.tensor_copy(dst, src)
+                codes = tile([P, step], U32, f"codes{z}{s}{h}_{j}")
+                scales = tile([P, step], U8, f"scales{z}{s}{h}_{j}")
+                nc.vector.quantize_mx(out=codes[:].bitcast(E4M3X4), scales=scales[:], in_=woven[:].bitcast(BF16))
+                for at in range(0, step, QUARTER):
+                    c = (h * width + j + at) // QUARTER
+                    quantised[z, s, c] = (codes[:, at : at + QUARTER], scales[:, at : at + QUARTER])
 
         def multiply(z, s, h):
-            width = J // PIECES[z]
-            codes, scales = quantised[z, s, h]
-            sc = dealt["scales"]
-            for cc in range(width // QW):
-                c = h * width // QW + cc
-                cols = slice(cc * QW, (cc + 1) * QW)
+            per_half = QUARTERS // HALVES[z]
+            for c in range(h * per_half, (h + 1) * per_half):
+                codes, scales = quantised[z, s, c]
                 for t in range(4):
                     if s == "a":
-                        lhsT = dealt["a"][:, z, t, :].bitcast(U8).bitcast(E2M1X4)
-                        lhsT_scale = sc[:, z, t, :]
+                        weight = dealt["a"][:, z, t, :].bitcast(U8).bitcast(E2M1X4)
+                        weight_scale = dealt["scales"][:, z, t, :]
                     else:
-                        lhsT = dealt["b"][:, z, t, :].bitcast(E4M3X4)
-                        lhsT_scale = sc[4:, z, t, :]
+                        weight = dealt["b"][:, z, t, :].bitcast(E4M3X4)
+                        weight_scale = dealt["scales"][WB_SCALE_ROW:, z, t, :]
                     nc.tensor.matmul_mx(
                         out=banks[s, c][:, t, :],
-                        lhsT=lhsT,
-                        lhsT_scale=lhsT_scale,
-                        rhs=codes[:, cols].bitcast(E4M3X4),
-                        rhs_scale=scales[:, cols],
+                        lhsT=weight,
+                        lhsT_scale=weight_scale,
+                        rhs=codes.bitcast(E4M3X4),
+                        rhs_scale=scales,
                         start=(z == 0 and t == 0),
                         stop=(z == PASSES - 1 and t == 3),
                     )
 
-        for z in range(PASSES):
-            for u in range(2):
-                gather_pair(z, u)
+        gather_first_pair(0, round_pair(0, 0))
+        deal_weight_scales()
+        gather_second_pair(0, round_pair(0, 1), 0)
+        for s in SIDES:
+            quantise(0, s, 0)
+        gather_first_pair(1, round_pair(1, 0))
+        deal_weight_codes()
+        for s in SIDES:
+            multiply(0, s, 0)
+        last_window = round_pair(1, 1)
+        for h in range(HALVES[1]):
+            gather_second_pair(1, last_window, h)
+            for s in SIDES:
+                quantise(1, s, h)
+            for s in SIDES:
+                multiply(1, s, h)
 
         y_codes = tile([P, J], U32, "y_codes")
         y_scales = tile([P, J], U8, "y_scales")
         out_rows = out_0.rearrange("(p t) j -> p t j", t=4)
         out_words = out_1[0].rearrange("p j r -> p (j r)").bitcast(I32)
         for c in range(QUARTERS):
-            cols = slice(c * QW, (c + 1) * QW)
-            mag = tile([P, 4, QW], F32, f"mag{c}")
-            nc.scalar.activation(mag[:], banks["b", c][:], ACT.Abs)
-            root = tile([P, 4, QW], F32, f"root{c}")
-            nc.scalar.activation(root[:], mag[:], ACT.Abs_reciprocal_sqrt, bias=one[:])
-            y = tile([P, 4, QW], F32, f"y{c}")
-            parts = 2 if c == QUARTERS - 1 else 1
-            w = QW // parts
-            for i in range(parts):
-                js = slice(i * w, (i + 1) * w)
-                recip = tile([P, 4, w], F32, f"recip{c}{i}")
-                soft = tile([P, 4, w], F32, f"soft{c}{i}")
-                nc.scalar.activation(recip[:], root[:, :, js], ACT.Square)
-                nc.vector.tensor_tensor(soft[:], banks["b", c][:, :, js], recip[:], MULT)
-                nc.vector.tensor_tensor(y[:, :, js], banks["a", c][:, :, js], soft[:], MULT)
-                yb = tile([P, w, 4], BF16, f"yb{c}{i}")
-                src = y[:, :, js].rearrange("p t (g e) -> p g t e", e=4)
-                dst = yb[:].rearrange("p (g e) t -> p g t e", e=4)
-                if (c, i) in ((2, 0), (3, 0)):
+            cols = slice(c * QUARTER, (c + 1) * QUARTER)
+            magnitude = tile([P, 4, QUARTER], F32, f"magnitude{c}")
+            nc.scalar.activation(magnitude[:], banks["b", c][:], ACT.Abs)
+            root = tile([P, 4, QUARTER], F32, f"root{c}")
+            nc.scalar.activation(root[:], magnitude[:], ACT.Abs_reciprocal_sqrt, bias=one[:])
+            y = tile([P, 4, QUARTER], F32, f"y{c}")
+            step = QUARTER // 2 if c == QUARTERS - 1 else QUARTER
+            for j in range(0, QUARTER, step):
+                part = slice(j, j + step)
+                reciprocal = tile([P, 4, step], F32, f"reciprocal{c}_{j}")
+                softsign = tile([P, 4, step], F32, f"softsign{c}_{j}")
+                nc.scalar.activation(reciprocal[:], root[:, :, part], ACT.Square)
+                nc.vector.tensor_tensor(softsign[:], banks["b", c][:, :, part], reciprocal[:], MULT)
+                nc.vector.tensor_tensor(y[:, :, part], banks["a", c][:, :, part], softsign[:], MULT)
+                rounded = tile([P, step, 4], BF16, f"rounded{c}_{j}")
+                src = y[:, :, part].rearrange("p t (g i) -> p g t i", i=LINE // 4)
+                dst = rounded[:].rearrange("p (g i) t -> p g t i", i=LINE // 4)
+                if c >= QUARTERS // 2 and j == 0:
                     nc.scalar.copy(dst, src)
                 else:
                     nc.vector.tensor_copy(dst, src)
-                oc = slice(c * QW + i * w, c * QW + (i + 1) * w)
+                slots = slice(c * QUARTER + j, c * QUARTER + j + step)
                 nc.vector.quantize_mx(
-                    out=y_codes[:, oc].bitcast(E4M3X4),
-                    scales=y_scales[:, oc],
-                    in_=yb[:].rearrange("p j t -> p (j t)"),
+                    out=y_codes[:, slots].bitcast(E4M3X4),
+                    scales=y_scales[:, slots],
+                    in_=rounded[:].rearrange("p j t -> p (j t)"),
                 )
             nc.sync.dma_start(out_rows[:, :, cols], y[:])
             nc.sync.dma_start(out_words[:, cols], y_codes[:, cols].bitcast(I32))
-        for q in range(4):
-            eng = nc.sync if q % 2 == 0 else nc.scalar
-            eng.dma_start(
-                out_2[0, 4 * q : 4 * q + 4, :].bitcast(I32), y_scales[32 * q : 32 * q + 4, :].bitcast(I32)
+        for quadrant in range(4):
+            queue = nc.sync if quadrant % 2 == 0 else nc.scalar
+            queue.dma_start(
+                out_2[0, 4 * quadrant : 4 * quadrant + 4, :].bitcast(I32),
+                y_scales[32 * quadrant : 32 * quadrant + 4, :].bitcast(I32),
             )

from contextlib import ExitStack

import concourse.mybir as mybir

K, T, J, N = 1024, 2048, 512, 512
FLOPS = 2 * 2 * K * J * N

F32 = mybir.dt.float32
BF16 = mybir.dt.bfloat16
I32 = mybir.dt.int32
U32 = mybir.dt.uint32
U16 = mybir.dt.uint16
U8 = mybir.dt.uint8
E4M3X4 = mybir.dt.float8_e4m3fn_x4
E2M1X4 = mybir.dt.float4_e2m1fn_x4
ACT = mybir.ActivationFunctionType
MULT = mybir.AluOpType.mult

P = 128
PASSES = K // 512
QUARTER = 128
QUARTERS = J // QUARTER
LINE = 16
SIDES = "ba"
WB_SCALE_ROW = 4

LOADS = {
    (0, 0): [(0, 2048, 1280)],
    (0, 1): [(0, 1024, 0), (1024, 1024, 704)],
    (1, 0): [(0, 1024, 0), (1024, 1024, 256)],
    (1, 1): [(0, 1024, 0), (1024, 768, 512), (1792, 256, 256)],
}
OVERLAP = 576
HALVES = (1, 2)
ROWS = {
    (0, "b", 0): (0, 2),
    (0, "a", 0): (1, 3),
    (1, "b", 0): (0, 4),
    (1, "a", 0): (2, 5),
    (1, "b", 1): (1, 2),
    (1, "a", 1): (3, 5),
}


def tile_list_product_of_two_picks_pl_kernel(
    tc, xt, wa_words, wa_scales, wb_words, wb_scales, offs, offs2, out_0, out_1, out_2
):
    nc = tc.nc
    with ExitStack() as ctx:
        pool = ctx.enter_context(tc.tile_pool(name="keep", bufs=1))
        psum = ctx.enter_context(tc.psum_pool(name="psum", bufs=1))

        def tile(shape, dtype, name, tag=None):
            return pool.tile(shape, dtype, name=name, tag=tag or name, align_bytes=64)

        lists = {"a": tile([P, J // 16], U16, "list_a"), "b": tile([P, J // 16], U16, "list_b")}

        unit = tile([P, 1], F32, "unit")
        nc.vector.memset(unit[:], 1.0)
        one = tile([P, 1], F32, "one")
        nc.scalar.activation(one[:], unit[:], ACT.Abs_reciprocal_sqrt)

        scales_raw = tile([P, PASSES, N // 4], I32, "scales_raw")
        nc.vector.memset(scales_raw[:], 0)
        wb_raw = tile([P, PASSES, N], I32, "wb_raw")
        wa_raw = tile([P, PASSES, N // 2], I32, "wa_raw")
        raw = {}

        def load_tokens(z, u, i):
            first, count, on_vector = LOADS[z, u][i]
            rows = xt[512 * z : 512 * (z + 1), :].rearrange("(p u e) c -> p u e c", u=2, e=2)
            raw[z, u, first] = tile([P, 2, count], F32, f"raw{z}{u}_{first}")
            nc.sync.dma_start(raw[z, u, first][:], rows[:, u, :, first : first + count])

        def load_weight_scales(quadrant):
            for row, source in ((0, wa_scales), (WB_SCALE_ROW, wb_scales)):
                at = 32 * quadrant + row
                nc.sync.dma_start(
                    scales_raw[at : at + 4, :, :],
                    source[:, 4 * quadrant : 4 * quadrant + 4, :].rearrange("z r n -> r z n").bitcast(I32),
                )

        load_tokens(0, 0, 0)
        nc.sync.dma_start(lists["b"][:], offs2)
        nc.sync.dma_start(lists["a"][:], offs)
        load_weight_scales(0)
        load_weight_scales(1)
        load_tokens(0, 1, 0)
        load_weight_scales(2)
        load_weight_scales(3)
        load_tokens(0, 1, 1)
        load_tokens(1, 0, 0)
        load_tokens(1, 0, 1)
        nc.sync.dma_start(wb_raw[:], wb_words.rearrange("z p n r -> p z (n r)").bitcast(I32))
        nc.sync.dma_start(wa_raw[:], wa_words.rearrange("z p b -> p z b").bitcast(I32))
        for i in range(len(LOADS[1, 1])):
            load_tokens(1, 1, i)

        dealt = {}

        def deal(dst, src, item_bytes):
            run = LINE // item_bytes
            nc.vector.tensor_copy(
                dst.rearrange("p z t (g i) -> p z g t i", i=run),
                src.rearrange("p z (g i t) -> p z g t i", i=run, t=4),
            )

        def deal_weight_scales():
            scales = tile([P, PASSES, 4, P], U8, "weight_scales", tag="raw00_0")
            dealt["scales"] = scales
            deal(scales[:], scales_raw[:].bitcast(U8), 1)

        def deal_weight_codes():
            both = tile([P, PASSES * (N + N // 2)], I32, "weight_codes", tag="raw10_1024")
            dealt["b"] = both[:, : PASSES * N].rearrange("p (z t m) -> p z t m", z=PASSES, t=4)
            dealt["a"] = both[:, PASSES * N :].bitcast(U16).rearrange("p (z t m) -> p z t m", z=PASSES, t=4)
            deal(dealt["b"], wb_raw[:], 4)
            deal(dealt["a"], wa_raw[:].bitcast(U16), 2)

        banks = {
            (s, c): psum.tile([P, 4, QUARTER], F32, name=f"bank_{s}{c}") for s in SIDES for c in range(QUARTERS)
        }
        windows = tile([P, 2 * (4 * T - 3 * OVERLAP)], BF16, "windows")
        picked, quantised = {}, {}

        def round_pair(z, u):
            start = (3 - 2 * z - u) * (T - OVERLAP)
            window = windows[:, 2 * start : 2 * (start + T)]
            for first, count, on_vector in LOADS[z, u]:
                src = raw[z, u, first][:].rearrange("p e c -> p c e")
                dst = window[:, 2 * first : 2 * (first + count)].rearrange("p (c e) -> p c e", e=2)
                split = count - on_vector
                if split:
                    nc.scalar.activation(dst[:, :split, :], src[:, :split, :], ACT.Copy)
                if on_vector:
                    nc.vector.tensor_copy(dst[:, split:, :], src[:, split:, :])
            return window.bitcast(F32)

        def gather_first_pair(z, window):
            picked[z] = tile([P, 2 * J + 2 * (J // HALVES[z])], F32, f"picked{z}")
            for i, s in enumerate(SIDES):
                nc.vector.tensor_copy(picked[z][:, i * J : (i + 1) * J], window.indirect(lists[s][:]))

        def gather_second_pair(z, window, h):
            width = J // HALVES[z]
            for s in SIDES:
                at = ROWS[z, s, h][1] * width
                entries = lists[s][:, h * width // 16 : (h + 1) * width // 16]
                nc.vector.tensor_copy(picked[z][:, at : at + width], window.indirect(entries))

        def quantise(z, s, h):
            width = J // HALVES[z]
            step = QUARTER if (z, s, h) == (PASSES - 1, "b", 0) else width
            row0, row1 = ROWS[z, s, h]
            rows = picked[z][:].rearrange("p (r j) -> p r j", j=width)[:, row0 : row1 + 1 : row1 - row0, :]
            for j in range(0, width, step):
                woven = tile([P, 2 * step], F32, f"woven{z}{s}{h}_{j}")
                src = rows[:, :, j : j + step].rearrange("p u j -> p j u")
                dst = woven[:].rearrange("p (j u) -> p j u", u=2)
                if (z, h) == (PASSES - 1, 0):
                    nc.scalar.copy(dst, src)
                else:
                    nc.vector.tensor_copy(dst, src)
                codes = tile([P, step], U32, f"codes{z}{s}{h}_{j}")
                scales = tile([P, step], U8, f"scales{z}{s}{h}_{j}")
                nc.vector.quantize_mx(out=codes[:].bitcast(E4M3X4), scales=scales[:], in_=woven[:].bitcast(BF16))
                for at in range(0, step, QUARTER):
                    c = (h * width + j + at) // QUARTER
                    quantised[z, s, c] = (codes[:, at : at + QUARTER], scales[:, at : at + QUARTER])

        def multiply(z, s, h):
            per_half = QUARTERS // HALVES[z]
            for c in range(h * per_half, (h + 1) * per_half):
                codes, scales = quantised[z, s, c]
                for t in range(4):
                    if s == "a":
                        weight = dealt["a"][:, z, t, :].bitcast(U8).bitcast(E2M1X4)
                        weight_scale = dealt["scales"][:, z, t, :]
                    else:
                        weight = dealt["b"][:, z, t, :].bitcast(E4M3X4)
                        weight_scale = dealt["scales"][WB_SCALE_ROW:, z, t, :]
                    nc.tensor.matmul_mx(
                        out=banks[s, c][:, t, :],
                        lhsT=weight,
                        lhsT_scale=weight_scale,
                        rhs=codes.bitcast(E4M3X4),
                        rhs_scale=scales,
                        start=(z == 0 and t == 0),
                        stop=(z == PASSES - 1 and t == 3),
                    )

        gather_first_pair(0, round_pair(0, 0))
        deal_weight_scales()
        gather_second_pair(0, round_pair(0, 1), 0)
        for s in SIDES:
            quantise(0, s, 0)
        gather_first_pair(1, round_pair(1, 0))
        deal_weight_codes()
        for s in SIDES:
            multiply(0, s, 0)
        last_window = round_pair(1, 1)
        for h in range(HALVES[1]):
            gather_second_pair(1, last_window, h)
            for s in SIDES:
                quantise(1, s, h)
            for s in SIDES:
                multiply(1, s, h)

        y_codes = tile([P, J], U32, "y_codes")
        y_scales = tile([P, J], U8, "y_scales")
        out_rows = out_0.rearrange("(p t) j -> p t j", t=4)
        out_words = out_1[0].rearrange("p j r -> p (j r)").bitcast(I32)
        for c in range(QUARTERS):
            cols = slice(c * QUARTER, (c + 1) * QUARTER)
            magnitude = tile([P, 4, QUARTER], F32, f"magnitude{c}")
            nc.scalar.activation(magnitude[:], banks["b", c][:], ACT.Abs)
            root = tile([P, 4, QUARTER], F32, f"root{c}")
            nc.scalar.activation(root[:], magnitude[:], ACT.Abs_reciprocal_sqrt, bias=one[:])
            y = tile([P, 4, QUARTER], F32, f"y{c}")
            step = QUARTER // 2 if c == QUARTERS - 1 else QUARTER
            for j in range(0, QUARTER, step):
                part = slice(j, j + step)
                reciprocal = tile([P, 4, step], F32, f"reciprocal{c}_{j}")
                softsign = tile([P, 4, step], F32, f"softsign{c}_{j}")
                nc.scalar.activation(reciprocal[:], root[:, :, part], ACT.Square)
                nc.vector.tensor_tensor(softsign[:], banks["b", c][:, :, part], reciprocal[:], MULT)
                nc.vector.tensor_tensor(y[:, :, part], banks["a", c][:, :, part], softsign[:], MULT)
                rounded = tile([P, step, 4], BF16, f"rounded{c}_{j}")
                src = y[:, :, part].rearrange("p t (g i) -> p g t i", i=LINE // 4)
                dst = rounded[:].rearrange("p (g i) t -> p g t i", i=LINE // 4)
                if c >= QUARTERS // 2 and j == 0:
                    nc.scalar.copy(dst, src)
                else:
                    nc.vector.tensor_copy(dst, src)
                slots = slice(c * QUARTER + j, c * QUARTER + j + step)
                nc.vector.quantize_mx(
                    out=y_codes[:, slots].bitcast(E4M3X4),
                    scales=y_scales[:, slots],
                    in_=rounded[:].rearrange("p j t -> p (j t)"),
                )
            nc.sync.dma_start(out_rows[:, :, cols], y[:])
            nc.sync.dma_start(out_words[:, cols], y_codes[:, cols].bitcast(I32))
        for quadrant in range(4):
            queue = nc.sync if quadrant % 2 == 0 else nc.scalar
            queue.dma_start(
                out_2[0, 4 * quadrant : 4 * quadrant + 4, :].bitcast(I32),
                y_scales[32 * quadrant : 32 * quadrant + 4, :].bitcast(I32),
            )
